import numpy as np
import ml_dtypes


def mxq(x, axis, fmt="e4m3"):
    dtype, down = {"e4m3": (ml_dtypes.float8_e4m3fn, 7), "e5m2": (ml_dtypes.float8_e5m2, 14)}[fmt]
    v = np.moveaxis(np.asarray(x, np.float32).astype(ml_dtypes.bfloat16).astype(np.float64), axis, -1)
    blocks = v.reshape(v.shape[:-1] + (-1, 32))
    amax = np.abs(blocks).max(-1, keepdims=True)
    byte = np.maximum(np.where(amax > 0, np.frexp(amax)[1] - 1 + 127, 0) - down, 1)
    scale = np.exp2(byte - 127.0)
    codes = (blocks / scale).astype(np.float32).astype(dtype).astype(np.float64)
    return np.moveaxis((codes * scale).reshape(v.shape), -1, axis)


WIDE = False


def mx_kscale(k):
    if not WIDE:
        return np.ones(k)
    levels = np.array([10, -10, 5, -5, 0])
    if k % 512:
        return np.exp2(np.random.permutation(np.resize(levels, k // 32))).repeat(32)
    a = np.empty((k // 512, 16))
    for p in range(k // 512):
        a[p, :8] = np.random.permutation(np.resize(levels, 8))
        for g in range(8):
            far = levels[np.abs(levels - a[p, g]) >= 10]
            a[p, g + 8] = far[np.random.randint(len(far))]
    return np.exp2(a.ravel()).repeat(32)


def f64(x):
    return np.asarray(x).astype(np.float64)


def striped(idx):
    return np.tile(idx.reshape(-1, 16).T, (8, 1)).astype(np.uint16)


def unstriped(offs):
    return offs[:16].T.reshape(-1).astype(np.int64)


def striped8(idx):
    return np.concatenate([x.reshape(-1, 16).T for x in idx]).astype(np.uint16)


def runs(offs, k):
    lists = np.stack([offs[16 * r : 16 * r + 16].T.reshape(-1) for r in range(8)]).astype(np.int64)
    return lists[np.arange(k) % 512 // 64]


def pack_weight(w):
    k, n = w.shape
    w = f64(np.asarray(w, np.float32).astype(ml_dtypes.bfloat16)).reshape(k // 32, 32, n)
    amax = np.abs(w).max(1)
    byte = np.clip(np.where(amax > 0, np.frexp(amax)[1] - 1 + 127 - 7, 1), 1, 254)
    scaled = (w * np.exp2(127.0 - byte)[:, None, :]).reshape(k, n).astype(np.float32)
    words = np.ascontiguousarray(scaled.reshape(k // 512, 128, 4, n).transpose(0, 1, 3, 2)).astype(ml_dtypes.float8_e4m3fn).view(np.uint8)
    return words, np.ascontiguousarray(byte.astype(np.uint8).reshape(k // 512, 16, n))


def unpack_weight(words, scales):
    g, p, n, _ = words.shape
    vals = np.ascontiguousarray(words).view(ml_dtypes.float8_e4m3fn).astype(np.float64) * np.repeat(np.exp2(scales.astype(np.float64) - 127.0), 8, axis=1)[..., None]
    return vals.transpose(0, 1, 3, 2).reshape(g * 512, n)


K, T, S, N, H = 512, 2048, 512, 512, 512


def setup_inputs():
    n = np.random.standard_normal
    s = mx_kscale(K)[:, None]
    u = mx_kscale(S)
    packed_xT = pack_weight(n((K, T)) * s)
    return {
        "x_words": packed_xT[0],
        "x_scales": packed_xT[1],
        "wa": (n((K, H)) / np.sqrt(K) / s).astype(np.float32),
        "wb": (n((K, H)) / np.sqrt(K) / s).astype(np.float32),
        "gt": (np.random.uniform(0.5, 1.5, (S, 1)) * u[:, None]).astype(np.float32),
        "w1": (n((S, N)) / np.sqrt(S) / u[:, None]).astype(np.float32),
        "offs": striped(np.random.permutation(T)[:S]),
        "two": striped(np.random.permutation(T)[:S]),
        "fl": striped8(np.stack([np.random.permutation(H) for _ in range(8)])),
    }


def reference(x_words, x_scales, wa, wb, gt, w1, offs, two, fl):
    xq = unpack_weight(x_words, x_scales)[:, unstriped(offs)]
    a = xq.T @ mxq(f64(wa), 0, "e4m3")
    x_two = unpack_weight(x_words, x_scales)[:, unstriped(two)]
    b = x_two.T @ mxq(f64(wb), 0, "e4m3")
    bq = b[np.arange(S)[:, None], runs(fl, S)]
    z = f64(gt) * np.maximum(a, bq)
    return mxq(f64(w1), 0, "e4m3").T @ mxq(z, 0, "e4m3")

from contextlib import ExitStack

import concourse.mybir as mybir

K, T, S, N, H = 512, 2048, 512, 512, 512
FLOPS = 2 * K * S * H * 2 + 2 * S * N * H

F32 = mybir.dt.float32
BF16 = mybir.dt.bfloat16
I32 = mybir.dt.int32
U32 = mybir.dt.uint32
U16 = mybir.dt.uint16
U8 = mybir.dt.uint8
FP8X4 = mybir.dt.float8_e4m3fn_x4
COPY = mybir.ActivationFunctionType.Copy
MAX = mybir.AluOpType.max
MULT = mybir.AluOpType.mult
ADD = mybir.AluOpType.add

P = 128
PACK = 4
RUN = 8
HALF = 256
CHUNK = 128
LIST_COLS = 16


def tile_picked_tokmax_none_p_kernel(
    tc, x_words, x_scales, wa, wb, gt, w1, offs, two, fl, out
):
    nc = tc.nc
    with ExitStack() as ctx:
        keep = ctx.enter_context(tc.tile_pool(name="keep", bufs=1))
        psum = ctx.enter_context(tc.psum_pool(name="psum", bufs=1))

        def held(name, shape, dtype):
            return keep.tile(shape, dtype, name=name, align_bytes=64)

        two_t = held("two_t", [P, S // LIST_COLS], U16)
        offs_t = held("offs_t", [P, S // LIST_COLS], U16)
        fl_t = held("fl_t", [P, H // LIST_COLS], U16)
        scale_win = held("scale_win", [P, T], U8)
        word_win = held("word_win", [P, T], I32)
        gt_t = held("gt_t", [P, PACK, 8], F32)

        nc.vector.memset(scale_win[:].bitcast(I32), 0)
        nc.sync.dma_start(two_t[:], two)
        nc.sync.dma_start(offs_t[:], offs)
        nc.sync.dma_start(fl_t[:], fl)
        for quad in range(4):
            nc.sync.dma_start(
                scale_win[32 * quad : 32 * quad + 4, :].bitcast(I32),
                x_scales[0, 4 * quad : 4 * quad + 4, :].bitcast(I32),
            )
        nc.sync.dma_start(word_win[:], x_words[0].rearrange("p c r -> p (c r)").bitcast(I32))

        def load_half(name, w, h):
            raw = held(name, [P, PACK, HALF], F32)
            nc.sync.dma_start(raw[:], w[:, h * HALF : (h + 1) * HALF].rearrange("(p j) n -> p j n", j=PACK))
            return raw

        wb_raw = [load_half("wb_raw%d" % h, wb, h) for h in range(2)]
        wa_raw = [load_half("wa_raw%d" % h, wa, h) for h in range(2)]
        w1_raw = held("w1_raw", [P, PACK, N], F32)
        w1_rows = w1.rearrange("(q t r) m -> t q r m", t=PACK, r=RUN)
        for t in range(PACK):
            nc.sync.dma_start(w1_raw[:, t, :], w1_rows[t])
        gt_rows = gt.rearrange("(q t r) o -> t q r o", t=PACK, r=RUN)
        with nc.allow_non_contiguous_dma(reason="one weight per place and partition"):
            for t in range(PACK):
                nc.sync.dma_start(gt_t[:, t, 0:1], gt_rows[t])

        def weave_views(dst, src):
            return (
                dst.rearrange("p (c i) t -> p c t i", i=4),
                src.rearrange("p t (c i) -> p c t i", i=4),
            )

        def weave_vector(dst, src):
            d, s = weave_views(dst, src)
            nc.vector.tensor_copy(out=d, in_=s)

        def weave_scalar(dst, src):
            d, s = weave_views(dst, src)
            nc.scalar.activation(out=d, in_=s, func=COPY)

        def quantize(name, woven, width, tag=""):
            codes = keep.tile([P, width], U32, name=name + "_codes", tag=tag, align_bytes=64)
            scales = held(name + "_scales", [P, width], U8)
            nc.vector.quantize_mx(
                out=codes[:].bitcast(FP8X4), scales=scales[:], in_=woven.rearrange("p n t -> p (n t)")
            )
            return codes, scales

        def product(dst, lhs, lhs_cols, rhs, rhs_cols):
            nc.tensor.matmul_mx(
                out=dst,
                lhsT=lhs[0][:, lhs_cols].bitcast(FP8X4),
                lhsT_scale=lhs[1][:, lhs_cols],
                rhs=rhs[0][:, rhs_cols].bitcast(FP8X4),
                rhs_scale=rhs[1][:, rhs_cols],
                start=True,
                stop=True,
            )

        picked = held("picked", [P, 2 * S], U8)
        nc.vector.tensor_copy(picked[:, :S], scale_win[:].indirect(two_t[:]))
        nc.vector.tensor_copy(picked[:, S:], scale_win[:].indirect(offs_t[:]))
        dealt = held("dealt", [P, 2 * S], U8)
        nc.vector.tensor_copy(
            out=dealt[:].bitcast(I32).rearrange("p (l t q w) -> p l t q w", l=2, t=PACK, w=RUN // 4),
            in_=picked[:].bitcast(I32).rearrange("p (l q t w) -> p l t q w", l=2, t=PACK, w=RUN // 4),
        )

        def pick_words(name, places):
            words = held(name + "_words", [P, S], U32)
            nc.vector.tensor_copy(
                words[:].rearrange("p (t q r) -> p q t r", t=PACK, r=RUN),
                word_win[:].bitcast(U32).indirect(places[:]),
            )
            return words

        xb = (pick_words("xb", two_t), dealt[:, :S])
        xa = (pick_words("xa", offs_t), dealt[:, S:])

        halves = [slice(0, HALF), slice(HALF, 2 * HALF)]
        wb_woven0 = held("wb_woven0", [P, HALF, PACK], BF16)
        wb_woven1 = keep.tile([P, HALF, PACK], BF16, name="wb_woven1", tag="wb_then_wa", align_bytes=64)
        weave_scalar(wb_woven0[:], wb_raw[0][:])
        weave_scalar(wb_woven1[:], wb_raw[1][:])
        wb_q = [quantize("wb0", wb_woven0[:], HALF), quantize("wb1", wb_woven1[:], HALF, tag="wb_then_w1")]
        wa_woven0 = held("wa_woven0", [P, HALF, PACK], BF16)
        weave_scalar(wa_woven0[:], wa_raw[0][:])
        wa_q = [quantize("wa0", wa_woven0[:], HALF)]
        wa_woven1 = keep.tile([P, HALF, PACK], BF16, name="wa_woven1", tag="wb_then_wa", align_bytes=64)
        weave_vector(wa_woven1[:], wa_raw[1][:])
        wa_q.append(quantize("wa1", wa_woven1[:], HALF))

        b_rows = []
        for t in range(PACK):
            b_ps = psum.tile([P, H], F32, name="b_ps", tag="b_or_out", bufs=4)
            for h in range(2):
                product(b_ps[:, halves[h]], xb, slice(t * P, (t + 1) * P), wb_q[h], slice(0, HALF))
            b_t = held("b_rows%d" % t, [P, H], F32)
            nc.scalar.copy(out=b_t[:], in_=b_ps[:])
            b_rows.append(b_t)

        def look_up(bq, first, width):
            entries = slice(first // LIST_COLS, (first + width) // LIST_COLS)
            for t in range(PACK):
                nc.vector.tensor_copy(bq[:, t, :], b_rows[t][:].indirect(fl_t[:, entries]))

        def larger(c, bq, dst):
            a_ps = psum.tile([P, PACK, CHUNK], F32, name="a_ps", tag="a_ps", bufs=4)
            for t in range(PACK):
                product(a_ps[:, t, :], xa, slice(t * P, (t + 1) * P), wa_q[c // 2], slice(c % 2 * CHUNK, (c % 2 + 1) * CHUNK))
            nc.vector.tensor_tensor(out=dst, in0=bq, in1=a_ps[:], op=MAX)

        def weigh(z_planes, top):
            for t in range(PACK):
                nc.scalar.activation(out=z_planes[:, t, :], in_=top[:, t, :], func=COPY, scale=gt_t[:, t, 0:1])

        def weave_z(name, weave, z_planes, width):
            z_woven = held(name, [P, width, PACK], BF16)
            weave(z_woven[:], z_planes)
            return z_woven

        def mix(name, z_woven, first, width, copies):
            z_q = quantize(name, z_woven[:], width)
            result = held(name + "_result", [P, N // P, width], F32)
            per_bank = 512 // width
            for bank, copy_out in enumerate(copies):
                o_ps = psum.tile([P, per_bank, width], F32, name="o_ps", tag="b_or_out", bufs=4)
                for u in range(per_bank):
                    mt = bank * per_bank + u
                    product(o_ps[:, u, :], w1_q, slice(mt * P, (mt + 1) * P), z_q, slice(0, width))
                rows = slice(bank * per_bank, (bank + 1) * per_bank)
                copy_out(out=result[:, rows, :], in_=o_ps[:])
                nc.sync.dma_start(
                    out[:, first : first + width].rearrange("(mt p) j -> p mt j", p=P)[:, rows, :], result[:, rows, :]
                )

        lo, hi = slice(0, CHUNK), slice(CHUNK, HALF)
        bq = held("bq", [P, PACK, HALF], F32)
        top_a = held("top_a", [P, PACK, HALF], F32)
        top_b = held("top_b", [P, PACK, CHUNK], F32)
        top_c = held("top_c", [P, PACK, CHUNK], F32)
        look_up(bq, 0, HALF)
        larger(0, bq[:, :, lo], top_a[:, :, lo])
        larger(1, bq[:, :, hi], top_a[:, :, hi])
        w1_woven = keep.tile([P, N, PACK], BF16, name="w1_woven", tag="wb_then_w1", align_bytes=64)
        for h in range(2):
            weave_scalar(w1_woven[:, halves[h], :], w1_raw[:, :, halves[h]])
        w1_q = quantize("w1", w1_woven[:], N)
        look_up(bq[:, :, lo], HALF, CHUNK)
        larger(2, bq[:, :, lo], top_b[:])
        look_up(bq[:, :, hi], HALF + CHUNK, CHUNK)
        larger(3, bq[:, :, hi], top_c[:])
        planes_a = keep.tile([P, PACK, HALF], BF16, name="planes_a", tag="planes", align_bytes=64)
        weigh(planes_a, top_a)
        woven_a = weave_z("woven_a", weave_scalar, planes_a[:], HALF)
        planes_bc = keep.tile([P, 2, PACK, CHUNK], BF16, name="planes_bc", tag="planes", align_bytes=64)
        weigh(planes_bc[:, 0], top_b)
        weigh(planes_bc[:, 1], top_c)
        mix("za", woven_a, 0, HALF, [nc.scalar.copy, nc.scalar.copy])
        mix("zb", weave_z("woven_b", weave_vector, planes_bc[:, 0], CHUNK), HALF, CHUNK, [nc.scalar.copy])
        mix("zc", weave_z("woven_c", weave_vector, planes_bc[:, 1], CHUNK), HALF + CHUNK, CHUNK, [nc.vector.tensor_copy])
